import numpy as np
CORES = [49,52,55,57,60,63,65,68,71,73,76,79]
N = 12
T, SQ = 4096, 2048
def entries(a): return a.T.reshape(-1)
def pack(v, P): return np.ascontiguousarray(np.asarray(v, np.int32).reshape(-1, P).T)
def lists(rng, how):
    d = np.concatenate([[0], rng.integers(1 - SQ // 2, SQ // 2, N - 1), [int(rng.integers(1 - SQ // 2, 1))]])
    if how == "lag": d[1:] = -SQ
    if how == "lead": d[1:N] = SQ; d[N] = 0
    if how == "runs": m = int(rng.integers(1, N - 2)); d[m] = -abs(d[m]); d[m + 1] = d[m] + SQ; d[m + 2] = d[m]
    if how == "skew": t = int(rng.integers(2, N - 1)); d[1:] = rng.integers(SQ // 2 + 1, SQ - 1, N); d[t + 1:] *= -1; d[t] = d[t - 1] + d[t + 1]
    n = SQ + np.diff(d)
    F = np.zeros((N, T), np.int64)
    for r in range(N):
        o = rng.permutation(T)
        if how == "runs": o = (T // 16 * rng.permutation(16)[:, None] + np.arange(T // 16)).reshape(-1)
        if how == "skew": o = np.concatenate([[0, T - 1], 1 + rng.permutation(T - 2)])
        F[r, o[:n[r]]] = 1
    return {"fl": np.stack([pack(f, 16) for f in F])}
def setup_inputs(rng):
    return dict({"x": rng.standard_normal((N, 128, T), dtype=np.float32), "st": rng.standard_normal((N, 128, SQ), dtype=np.float32)}, **lists(rng, "uniform"))
def setup_inputs_lag(rng):
    d = setup_inputs(rng); d.update(lists(rng, "lag"))
    for k in ("x", "st"): d[k] = (d[k].astype(np.float32) * 1048576.0).astype(d[k].dtype)
    return d
def setup_inputs_lead(rng):
    d = setup_inputs(rng); d.update(lists(rng, "lead"))
    for k in ("x", "st"): d[k] = (d[k].astype(np.float32) * (1 / 1024.0)).astype(d[k].dtype)
    return d
def setup_inputs_runs(rng):
    d = setup_inputs(rng); d.update(lists(rng, "runs"))
    return d
def setup_inputs_skew(rng):
    d = setup_inputs(rng); d.update(lists(rng, "skew"))
    return d
def check_inputs(x):
    bad = []
    if x["fl"].min() < 0 or x["fl"].max() >= 2: bad.append("fl out of range")
    if int(x["fl"].sum()) > N * SQ: bad.append("more flags than the stream has columns")
    c = np.concatenate([[0], np.cumsum([int(a.sum()) for a in x["fl"]])])
    if any(c[r] < (r - 1) * SQ or c[r + 1] > (r + 2) * SQ for r in range(N)): bad.append("a rank's share of the stream reaches beyond its neighbours' parts")
    return bad
def reference(x, st, fl):
    S = np.concatenate(list(st), axis=1); X = np.concatenate(list(x), axis=1)
    F = np.concatenate([entries(f) for f in fl]) > 0; c = np.cumsum(F) - F
    Y = np.where(F[None, :], S[:, np.minimum(c, N * SQ - 1)], X)
    return {"y": np.stack([Y[:, T * r:T * r + T] for r in range(N)])}

from concourse.bass import DstId, RemoteDMATransfer
from concourse.mybir import AluOpType as Op, AxisListType, ActivationFunctionType as Fn

COLS, SQ = 4096, 2048
BLOCKS = [384, 640, 1024]

SCRATCH = {
    "win": ("sbuf", [128, COLS + 3 * SQ], "float32"),
    "yb": ("sbuf", [128, COLS], "float32"),
    "rb": ("sbuf", [128, SQ], "float32"),
    "fd": ("dram", [128, 32], "int32"),
    "hd": ("dram", [128, 32], "int32"),
    "cd": ("dram", [12 * 128, 32], "int32"),
    "cf": ("sbuf", [128, 12 * 32], "int32"),
    "cff": ("sbuf", [128, 12 * 32], "float32"),
    "cr": ("sbuf", [128, 1], "float32"),
    "flt": ("sbuf", [16, 256], "int32"),
    "f16": ("sbuf", [16, 256], "bfloat16"),
    "ja": ("sbuf", [16, 256], "bfloat16"),
    "jb": ("sbuf", [16, 256], "bfloat16"),
    "dv": ("sbuf", [16, 128], "float32"),
    "lm": ("sbuf", [16, 128], "bfloat16"),
    "rm": ("sbuf", [16, 128], "bfloat16"),
    "om": ("sbuf", [16, 128], "bfloat16"),
    "one": ("sbuf", [128, 256], "float32"),
    "sc": ("sbuf", [128, 256], "float32"),
    "d": ("sbuf", [128, 256], "float32"),
    "fv": ("sbuf", [128, 256], "float32"),
    "fc": ("sbuf", [128, 256], "float32"),
    "off": ("sbuf", [128, 256], "uint16"),
    "pS": ("psum", [128, 512], "float32"),
    "pP": ("psum", [128, 512], "float32"),
    "pF": ("psum", [128, 512], "float32"),
    "pJ": ("psum", [128, 512], "float32"),
    "pC": ("psum", [128, 512], "float32"),
}
SEMAPHORES = ["st0", "st1", "xl", "ys", "fdl", "fsl", "cdl", "fin", "hin", "din", "arr", "lf", "l0", "l1",
              "gi", "v", "t", "gv0", "gv1", "gv2", "gs0", "gs1", "gs2"]


def bits(mask):
    return [1 << b for b in range(mask.bit_length()) if (mask >> b) & 1]


def low_slot(r):
    return max(0, r - 1)


def slot(r, q):
    return COLS + SQ * (q - low_slot(r))


def split(src, dsts, topo):
    near = [d for d in dsts if topo.chip(d) == topo.chip(src)]
    far = [d for d in dsts if topo.chip(d) != topo.chip(src)]
    out, used = [], 0
    if far:
        used = topo.mask(src, far[0])
        out.append((used, far))
    if near:
        out.append((topo.mask(src, near[0]) & ~used, near))
    return out


def build(T, topo):
    cs = list(T.cores)
    n = len(cs)
    flag_port, pieces = {}, {}
    for q in range(n):
        c = cs[q]
        mine = [k for k in range(max(cs) + 1) if topo.chip(k) == topo.chip(c)]
        ports = [k for k in mine if T.rank_of(k) is None and all(topo.may_write(k, d) for d in cs)]
        here = [k for k in cs if topo.chip(k) == topo.chip(c)]
        if q < n - 1:
            flag_port[q] = ports[here.index(c)]
        nb = [p for p in (q - 1, q + 1) if 0 <= p < n]
        far = [p for p in nb if topo.chip(cs[p]) != topo.chip(c)]
        if far:
            same = [k for k in ports if topo.die(k) == topo.die(c)]
            if topo.may_write(c, cs[far[0]]):
                pieces[q] = [(same[0], 0, 896, nb), (c, 896, 1152, nb)]
            else:
                pieces[q] = [(same[0], 0, 1152, nb), (same[1], 1152, 896, nb)]
        else:
            pieces[q] = [(c, 0, 1024, nb), (c, 1024, 1024, nb)]
    arr, fin = {c: 0 for c in cs}, {c: 0 for c in cs}
    for q in range(n):
        for car, _, _, nb in pieces[q]:
            for mask, ds in piece_groups(car, [cs[p] for p in nb], topo):
                for d in ds:
                    arr[d] += len(bits(mask))
        if q in flag_port:
            for mask, ds in split(flag_port[q], cs[q + 1:], topo):
                for d in ds:
                    fin[d] += len(bits(mask))
    return cs, flag_port, pieces, arr, fin


def piece_groups(car, dsts, topo):
    gr = split(car, dsts, topo)
    if len(gr) == 1 and len(gr[0][1]) == 2:
        b = bits(gr[0][0])
        h = len(b) // 2
        gr = [(sum(b[:h]), gr[0][1][:1]), (sum(b[h:]), gr[0][1][1:])]
    return gr


def fused(g, topo, src_ap, groups, dst_of, rsem, lsem):
    tr = []
    for mask, ds in groups:
        ids = []
        for d in ds:
            rid, pid, _ = topo.addr(d)
            ids.append(DstId(rid=rid, pnc=pid))
        tr.append(RemoteDMATransfer(dst_ids=ids, dma_engine_mask=mask, remote_sem=rsem,
                                    srcs=[src_ap], dsts=[dst_of(d) for d in ds]))
    g.remote_dma_fused(tr, local_sem=lsem)
    return sum(len(bits(m)) for m, _ in groups)


def carrier_program(g, core, T, topo, plan):
    cs, flag_port, pieces, _, _ = plan
    left = 0
    for q in flag_port:
        if flag_port[q] == core:
            g.wait_ge(T.sem.hin, len(bits(topo.mask(cs[q], core))))
            left += fused(g, topo, T.hd[:], split(core, cs[q + 1:], topo),
                          lambda d, q=q: T.cd[128 * q:128 * q + 128, :], T.sem.fin, T.sem.l1)
    for q in pieces:
        for car, a, w, nb in pieces[q]:
            if car == core:
                g.wait_ge(T.sem.din, len(bits(topo.mask(cs[q], core))))
                for grp in piece_groups(core, [cs[p] for p in nb], topo):
                    left += fused(g, topo, T.rb[:, 0:w], [grp],
                                  lambda d, q=q, a=a, w=w: T.win[:, slot(T.rank_of(d), q) + a:slot(T.rank_of(d), q) + a + w],
                                  T.sem.arr, T.sem.l1)
    if left:
        g.wait_ge(T.sem.l1, left)


def rank_program(g, core, T, topo):
    plan = build(T, topo)
    cs, flag_port, pieces, arr, fin = plan
    r = T.rank_of(core)
    if r is None:
        carrier_program(g, core, T, topo, plan)
        return
    n = len(cs)
    S = T.sem
    own = slot(r, r)
    wide = COLS + SQ * (min(n - 1, r + 1) - low_slot(r) + 1)

    for i, (car, a, w, nb) in enumerate(pieces[r]):
        g.sync.dma_start(T.win[:, own + a:own + a + w], T.st[:, a:a + w]).then_inc(S["st%d" % i], 16)

    if r in flag_port:
        g.scalar.dma_start(T.fd[:], T.fl[:]).then_inc(S.fdl, 16)
    g.scalar.dma_start(T.flt[:], T.fl[:]).then_inc(S.fsl, 16)

    g.iota(T.dv[:], [[0, 8], [1, 16]], 0, -1, allow_small_or_imprecise_dtypes=True).then_inc(S.gi, 1)
    g.iota(T.ja[:], [[16, 256]], 0, 0, allow_small_or_imprecise_dtypes=True).then_inc(S.gi, 1)
    g.iota(T.jb[:], [[0, 256]], 0, 1, allow_small_or_imprecise_dtypes=True).then_inc(S.gi, 1)
    lf = 0
    if r in flag_port:
        p = flag_port[r]
        m = topo.mask(core, p)
        rid, pid, _ = topo.addr(p)
        g.wait_ge(S.fdl, 16)
        g.remote_dma(out_ap=T.hd[:], in_ap=T.fd[:], remote_sem=S.hin, local_sem=S.lf, pid=pid, routing_id=rid,
                     dma_engine_mask=m)
        lf = len(bits(m))
    left = []
    for i, (car, a, w, nb) in enumerate(pieces[r]):
        g.wait_ge(S["st%d" % i], 16)
        src = T.win[:, own + a:own + a + w]
        if car == core:
            k = fused(g, topo, src, piece_groups(core, [cs[p] for p in nb], topo),
                      lambda d: T.win[:, slot(T.rank_of(d), r) + a:slot(T.rank_of(d), r) + a + w], S.arr, S["l%d" % i])
        else:
            m = topo.mask(core, car)
            rid, pid, _ = topo.addr(car)
            g.remote_dma(out_ap=T.rb[:, 0:w], in_ap=src, remote_sem=S.din, local_sem=S["l%d" % i], pid=pid,
                         routing_id=rid, dma_engine_mask=m)
            k = len(bits(m))
        left.append(k)
    if lf:
        g.wait_ge(S.lf, lf)
    g.wait_ge(S.l1, left[1])

    g.sync.wait_ge(S.l0, left[0])
    g.sync.dma_start(T.win[:, 0:COLS], T.x[:]).then_inc(S.xl, 16)

    if r:
        g.scalar.wait_ge(S.fin, fin[core])
        g.scalar.dma_start(T.cf[:, 0:32 * r], T.cd[0:128 * r, :]).then_inc(S.cdl, 16)

    v = g.vector
    nv = [0]

    def step(ins):
        ins.then_inc(S.v, 1)
        nv[0] += 1
        v.wait_ge(S.v, nv[0])

    step(v.memset(T.one[:], 1.0))
    step(v.memset(T.om[:], 1.0))
    v.wait_ge(S.gi, 3)
    step(v.tensor_scalar(T.lm[:], T.dv[:], 0.0, -1.0, Op.is_gt, Op.add))
    step(v.tensor_scalar(T.rm[:], T.dv[:], 0.0, None, Op.is_equal))
    g.tensor.wait_ge(S.v, nv[0])
    g.tensor.wait_ge(S.gi, 3)
    g.tensor.matmul(T.pJ[:, 0:256], T.rm[:], T.ja[:], True, False)
    g.tensor.matmul(T.pJ[:, 0:256], T.rm[:], T.jb[:], False, True).then_inc(S.t, 1)
    v.wait_ge(S.fsl, 16)
    step(v.tensor_copy(T.f16[:], T.flt[:]))
    g.tensor.wait_ge(S.v, nv[0])
    g.tensor.matmul(T.pS[:, 0:256], T.om[:], T.f16[:], True, True).then_inc(S.t, 1)
    g.tensor.matmul(T.pP[:, 0:256], T.lm[:], T.f16[:], True, True).then_inc(S.t, 1)
    g.tensor.matmul(T.pF[:, 0:256], T.rm[:], T.f16[:], True, True).then_inc(S.t, 1)
    v.wait_ge(S.t, 4)
    step(v.tensor_tensor_scan(T.sc[:], T.one[:], T.pS[:, 0:256], float(COLS - SQ * low_slot(r)), Op.mult, Op.add))
    step(v.tensor_copy(T.fv[:], T.pF[:, 0:256]))
    step(v.tensor_tensor(T.d[:], T.sc[:], T.pP[:, 0:256], Op.add))
    step(v.tensor_tensor(T.d[:], T.d[:], T.pJ[:, 0:256], Op.subtract))
    step(v.tensor_tensor(T.d[:], T.d[:], T.fv[:], Op.mult))
    step(v.tensor_tensor(T.d[:], T.d[:], T.pJ[:, 0:256], Op.add))
    if r:
        v.wait_ge(S.cdl, 16)
        step(v.tensor_copy(T.cff[:, 0:32 * r], T.cf[:, 0:32 * r]))
        step(v.tensor_reduce(T.cr[:], T.cff[:, 0:32 * r], AxisListType.X, Op.add))
        g.tensor.wait_ge(S.v, nv[0])
        g.tensor.matmul(T.pC[:, 0:1], T.one[:, 0:128], T.cr[:], True, True).then_inc(S.t, 1)
        v.wait_ge(S.t, 5)
        step(v.tensor_scalar(T.fc[:], T.fv[:], T.pC[:, 0:1], None, Op.mult))
        step(v.tensor_tensor(T.d[:], T.d[:], T.fc[:], Op.add))
    step(v.tensor_copy(T.off[:], T.d[:]))

    g.scalar.wait_ge(S.v, nv[0])
    for e in (v, g.scalar):
        e.wait_ge(S.st0, 16)
        e.wait_ge(S.st1, 16)
        e.wait_ge(S.xl, 16)
        e.wait_ge(S.arr, arr[core])
    at = 0
    for i, w in enumerate(BLOCKS):
        b = at + w
        v.tensor_copy(T.yb[:, at:b], T.win[:, 0:wide].indirect(T.off[:, at // 16:b // 16])).then_inc(S["gv%d" % i], 1)
        g.scalar.activation(T.yb[:, b:b + w], T.win[:, 0:wide].indirect(T.off[:, b // 16:(b + w) // 16]),
                            Fn.Copy).then_inc(S["gs%d" % i], 1)
        g.sync.wait_ge(S["gv%d" % i], 1)
        g.sync.dma_start(T.y[:, at:b], T.yb[:, at:b]).then_inc(S.ys, 16)
        g.sync.wait_ge(S["gs%d" % i], 1)
        g.sync.dma_start(T.y[:, b:b + w], T.yb[:, b:b + w]).then_inc(S.ys, 16)
        at = b + w
    g.sync.wait_ge(S.ys, 32 * len(BLOCKS))
